import numpy as np
import ml_dtypes


def mxq(x, axis, fmt="e4m3"):
    dtype, down = {"e4m3": (ml_dtypes.float8_e4m3fn, 7), "e5m2": (ml_dtypes.float8_e5m2, 14)}[fmt]
    v = np.moveaxis(np.asarray(x, np.float32).astype(ml_dtypes.bfloat16).astype(np.float64), axis, -1)
    blocks = v.reshape(v.shape[:-1] + (-1, 32))
    amax = np.abs(blocks).max(-1, keepdims=True)
    byte = np.maximum(np.where(amax > 0, np.frexp(amax)[1] - 1 + 127, 0) - down, 1)
    scale = np.exp2(byte - 127.0)
    codes = (blocks / scale).astype(np.float32).astype(dtype).astype(np.float64)
    return np.moveaxis((codes * scale).reshape(v.shape), -1, axis)


WIDE = False


def mx_kscale(k):
    if not WIDE:
        return np.ones(k)
    levels = np.array([10, -10, 5, -5, 0])
    if k % 512:
        return np.exp2(np.random.permutation(np.resize(levels, k // 32))).repeat(32)
    a = np.empty((k // 512, 16))
    for p in range(k // 512):
        a[p, :8] = np.random.permutation(np.resize(levels, 8))
        for g in range(8):
            far = levels[np.abs(levels - a[p, g]) >= 10]
            a[p, g + 8] = far[np.random.randint(len(far))]
    return np.exp2(a.ravel()).repeat(32)


def f64(x):
    return np.asarray(x).astype(np.float64)


def striped(idx):
    return np.tile(idx.reshape(-1, 16).T, (8, 1)).astype(np.uint16)


def unstriped(offs):
    return offs[:16].T.reshape(-1).astype(np.int64)


def striped8(idx):
    return np.concatenate([x.reshape(-1, 16).T for x in idx]).astype(np.uint16)


def runs(offs, k):
    lists = np.stack([offs[16 * r : 16 * r + 16].T.reshape(-1) for r in range(8)]).astype(np.int64)
    return lists[np.arange(k) % 512 // 64]


def pack_weight(w):
    k, n = w.shape
    w = f64(np.asarray(w, np.float32).astype(ml_dtypes.bfloat16)).reshape(k // 32, 32, n)
    amax = np.abs(w).max(1)
    byte = np.clip(np.where(amax > 0, np.frexp(amax)[1] - 1 + 127 - 7, 1), 1, 254)
    scaled = (w * np.exp2(127.0 - byte)[:, None, :]).reshape(k, n).astype(np.float32)
    words = np.ascontiguousarray(scaled.reshape(k // 512, 128, 4, n).transpose(0, 1, 3, 2)).astype(ml_dtypes.float8_e4m3fn).view(np.uint8)
    return words, np.ascontiguousarray(byte.astype(np.uint8).reshape(k // 512, 16, n))


def unpack_weight(words, scales):
    g, p, n, _ = words.shape
    vals = np.ascontiguousarray(words).view(ml_dtypes.float8_e4m3fn).astype(np.float64) * np.repeat(np.exp2(scales.astype(np.float64) - 127.0), 8, axis=1)[..., None]
    return vals.transpose(0, 1, 3, 2).reshape(g * 512, n)


def relu(v):
    return np.maximum(v, 0.0)

def planes(y):
    n, m = y.shape
    v = y.astype(np.float32).astype(ml_dtypes.bfloat16).astype(np.float64).reshape(n // 32, 32, m)
    top = np.abs(v).max(1)
    byte = np.clip(np.where(top > 0, np.frexp(top)[1] - 1 + 127 - 7, 1), 1, 254)
    codes = (v * np.exp2(127.0 - byte)[:, None, :]).reshape(n, m).astype(np.float32).astype(ml_dtypes.float8_e4m3fn).view(np.uint8)
    words = codes.reshape(n // 512, 128, 4, m).transpose(0, 1, 3, 2)
    return np.ascontiguousarray(words), np.ascontiguousarray(byte.astype(np.uint8).reshape(n // 512, 16, m))


K, T, S, V, H = 512, 2048, 512, 256, 512


def setup_inputs():
    n = np.random.standard_normal
    s = mx_kscale(K)[:, None]
    packed_xT = pack_weight(n((K, T)) * s)
    packed_w1 = pack_weight(n((K, H)) / np.sqrt(K) / s)
    return {
        "x_words": packed_xT[0],
        "x_scales": packed_xT[1],
        "w1_words": packed_w1[0],
        "w1_scales": packed_w1[1],
        "gs": (np.random.uniform(0.5, 1.5, (K, 1)) / s).astype(np.float32),
        "offs": striped(np.random.permutation(T)[:S]),
        "l1": striped8(np.stack([np.random.permutation(S)[:V] for _ in range(8)])),
        "l2": striped8(np.stack([np.random.permutation(S)[:V] for _ in range(8)])),
        "cand": striped(np.random.permutation(T)[:S]),
    }


def reference(x_words, x_scales, w1_words, w1_scales, gs, offs, l1, l2, cand):
    x_cand = unpack_weight(x_words, x_scales)[:, unstriped(cand)]
    xq = unpack_weight(x_words, x_scales)[:, unstriped(offs)]
    h = relu(unpack_weight(w1_words, w1_scales).T @ xq)
    z = f64(gs) * (h[np.arange(H)[:, None], runs(l1, H)] - (h[np.arange(H)[:, None], runs(l2, H)]))
    out_0 = 0.0625 * ((x_cand.T @ mxq(z, 0, "e4m3")))
    return (out_0,) + planes(out_0)

@@ -1,0 +1,153 @@
+from contextlib import ExitStack
+
+import concourse.mybir as mybir
+
+K, T, S, V, H = 512, 2048, 512, 256, 512
+FLOPS = 2 * K * H * S + 2 * K * S * V
+
+F32 = mybir.dt.float32
+BF16 = mybir.dt.bfloat16
+I32 = mybir.dt.int32
+U32 = mybir.dt.uint32
+U16 = mybir.dt.uint16
+U8 = mybir.dt.uint8
+FP8X4 = mybir.dt.float8_e4m3fn_x4
+ACT = mybir.ActivationFunctionType
+ALU = mybir.AluOpType
+
+P = 128
+PACK = 4
+QUADS = 4
+HALF = V // 2
+LIST = 16
+OUT_SCALE = 0.0625
+
+
+def tile_picked_candpair8_none_po_kernel(
+    tc, x_words, x_scales, w1_words, w1_scales, gs, offs, l1, l2, cand, out_0, out_1, out_2
+):
+    nc = tc.nc
+    with ExitStack() as ctx:
+        keep = ctx.enter_context(tc.tile_pool(name="keep", bufs=1))
+        psum = ctx.enter_context(tc.psum_pool(name="psum", bufs=1))
+
+        def tile(name, shape, dtype, tag=""):
+            return keep.tile(shape, dtype, name=name, tag=tag or name, align_bytes=64)
+
+        offs_sb = tile("offs_sb", [P, S // LIST], U16)
+        cand_sb = tile("cand_sb", [P, S // LIST], U16)
+        l1_sb = tile("l1_sb", [P, V // LIST], U16)
+        l2_sb = tile("l2_sb", [P, V // LIST], U16)
+        xw = tile("xw", [P, T], I32)
+        xs = tile("xs", [P, T], U8)
+        ww = tile("ww", [P, H], I32)
+        ws = tile("ws", [P, H], U8)
+        gs_sb = tile("gs_sb", [P, PACK], F32)
+
+        nc.vector.memset(xs[:].bitcast(I32), 0)
+        nc.vector.memset(ws[:].bitcast(I32), 0)
+
+        nc.sync.dma_start(offs_sb[:], offs)
+        nc.sync.dma_start(cand_sb[:], cand)
+        for q in range(QUADS):
+            nc.sync.dma_start(xs[32 * q : 32 * q + 4, :].bitcast(I32), x_scales[0, 4 * q : 4 * q + 4, :].bitcast(I32))
+        nc.sync.dma_start(xw[:], x_words[0].rearrange("p n t -> p (n t)").bitcast(I32))
+        nc.sync.dma_start(ww[:], w1_words[0].rearrange("p n t -> p (n t)").bitcast(I32))
+        for q in range(QUADS):
+            nc.sync.dma_start(ws[32 * q : 32 * q + 4, :].bitcast(I32), w1_scales[0, 4 * q : 4 * q + 4, :].bitcast(I32))
+        nc.sync.dma_start(l2_sb[:], l2)
+        nc.sync.dma_start(l1_sb[:], l1)
+        nc.sync.dma_start(gs_sb[:], gs.rearrange("(p t) o -> p (t o)", t=PACK))
+
+        def dealt(ap):
+            return ap.rearrange("p (t m) -> p m t", t=PACK)
+
+        def plain(ap):
+            return ap.rearrange("p (m t) -> p m t", t=PACK)
+
+        qs = tile("qs", [P, S], U8)
+        nc.vector.tensor_copy(qs[:], xs[:].indirect(offs_sb[:]))
+        cs = tile("cs", [P, S], U8)
+        nc.vector.tensor_copy(cs[:], xs[:].indirect(cand_sb[:]))
+        qw = tile("qw", [P, S], U32)
+        nc.vector.tensor_copy(qw[:], xw[:].bitcast(U32).indirect(offs_sb[:]))
+        wwd = tile("wwd", [P, H], I32)
+        nc.vector.tensor_copy(dealt(wwd[:]), plain(ww[:]))
+        wsd = tile("wsd", [P, H], U8)
+        nc.vector.tensor_copy(dealt(wsd[:]), plain(ws[:]))
+        csd = tile("csd", [P, S], U8, tag="ws")
+        nc.vector.tensor_copy(dealt(csd[:]), plain(cs[:]))
+        cw = tile("cw", [P, S], U32, tag="cs")
+        nc.vector.tensor_copy(dealt(cw[:]), xw[:].bitcast(U32).indirect(cand_sb[:]))
+
+        h = []
+        for t in range(PACK):
+            cols = slice(t * P, (t + 1) * P)
+            acc = psum.tile([P, S], F32, name=f"acc{t}")
+            nc.tensor.matmul_mx(
+                out=acc[:],
+                lhsT=wwd[:, cols].bitcast(FP8X4),
+                lhsT_scale=wsd[:, cols],
+                rhs=qw[:].bitcast(FP8X4),
+                rhs_scale=qs[:],
+                start=True,
+                stop=True,
+            )
+            h_t = tile(f"h{t}", [P, S], F32)
+            nc.scalar.activation(h_t[:], acc[:], ACT.Relu)
+            h.append(h_t)
+
+        out_rows = out_0.rearrange("(p t) v -> p t v", t=PACK)
+        zb = [tile(f"zb{u}", [P, HALF, PACK], BF16) for u in range(2)]
+        for t in range(PACK):
+            seconds = []
+            for u in range(2):
+                entries = slice(u * HALF // LIST, (u + 1) * HALF // LIST)
+                second = tile(f"second{u}{t}", [P, HALF], F32)
+                nc.vector.tensor_copy(second[:], h[t][:].indirect(l2_sb[:, entries]))
+                seconds.append(second)
+            for u in range(2):
+                entries = slice(u * HALF // LIST, (u + 1) * HALF // LIST)
+                diff = tile(f"diff{u}{t}", [P, HALF], F32)
+                nc.vector.tensor_tensor(diff[:], h[t][:].indirect(l1_sb[:, entries]), seconds[u][:], ALU.subtract)
+                nc.scalar.activation(zb[u][:, :, t], diff[:], ACT.Copy, scale=gs_sb[:, t : t + 1])
+
+        banks = []
+        for u in range(2):
+            zw = tile(f"zw{u}", [P, HALF], U32)
+            zs = tile(f"zs{u}", [P, HALF], U8)
+            nc.vector.quantize_mx(out=zw[:].bitcast(FP8X4), scales=zs[:], in_=zb[u][:].rearrange("p v t -> p (v t)"))
+            bank = psum.tile([P, PACK * HALF], F32, name=f"bank{u}")
+            for t in range(PACK):
+                cols = slice(t * P, (t + 1) * P)
+                nc.tensor.matmul_mx(
+                    out=bank[:, t * HALF : (t + 1) * HALF],
+                    lhsT=cw[:, cols].bitcast(FP8X4),
+                    lhsT_scale=csd[:, cols],
+                    rhs=zw[:].bitcast(FP8X4),
+                    rhs_scale=zs[:],
+                    start=True,
+                    stop=True,
+                )
+            banks.append(bank)
+
+        ow = tile("ow", [P, V], I32)
+        osc = tile("osc", [P, V], U8)
+        y0 = tile("y0", [P, PACK, HALF], F32)
+        nc.scalar.activation(y0[:].rearrange("p t v -> p (t v)"), banks[0][:], ACT.Copy, scale=OUT_SCALE)
+        nc.sync.dma_start(out_rows[:, :, :HALF], y0[:])
+        yb1 = tile("yb1", [P, HALF, PACK], BF16)
+        nc.vector.tensor_scalar_mul(yb1[:], banks[1][:].rearrange("p (t v) -> p v t", t=PACK), OUT_SCALE)
+        for pair in range(2):
+            y1 = tile(f"y1{pair}", [P, 2, HALF], F32)
+            nc.scalar.activation(y1[:].rearrange("p e v -> p (e v)"), banks[1][:, pair * V : (pair + 1) * V], ACT.Copy, scale=OUT_SCALE)
+            nc.sync.dma_start(out_rows[:, 2 * pair : 2 * pair + 2, HALF:], y1[:])
+        yb0 = tile("yb0", [P, HALF, PACK], BF16)
+        nc.vector.tensor_copy(yb0[:], y0[:].rearrange("p t v -> p v t"))
+        for u, yb in ((1, yb1), (0, yb0)):
+            vcols = slice(u * HALF, (u + 1) * HALF)
+            nc.vector.quantize_mx(out=ow[:, vcols].bitcast(FP8X4), scales=osc[:, vcols], in_=yb[:].rearrange("p v t -> p (v t)"))
+        nc.scalar.dma_start(out_1[0].rearrange("p v r -> p (v r)").bitcast(I32), ow[:])
+        for q in range(QUADS):
+            queue = nc.sync if q % 2 == 0 else nc.scalar
+            queue.dma_start(out_2[0, 4 * q : 4 * q + 4, :].bitcast(I32), osc[32 * q : 32 * q + 4, :].bitcast(I32))

@@ -47,16 +47,19 @@ def tile_picked_candpair8_none_po_kernel(
         nc.vector.memset(xs[:].bitcast(I32), 0)
         nc.vector.memset(ws[:].bitcast(I32), 0)
 
-        nc.sync.dma_start(offs_sb[:], offs)
+        def load_scales(plane, rows, q):
+            nc.sync.dma_start(plane[32 * q : 32 * q + 4, :].bitcast(I32), rows[0, 4 * q : 4 * q + 4, :].bitcast(I32))
+
         nc.sync.dma_start(cand_sb[:], cand)
+        nc.sync.dma_start(offs_sb[:], offs)
         for q in range(QUADS):
-            nc.sync.dma_start(xs[32 * q : 32 * q + 4, :].bitcast(I32), x_scales[0, 4 * q : 4 * q + 4, :].bitcast(I32))
+            load_scales(xs, x_scales, q)
+        nc.sync.dma_start(l2_sb[:], l2)
+        nc.sync.dma_start(l1_sb[:], l1)
         nc.sync.dma_start(xw[:], x_words[0].rearrange("p n t -> p (n t)").bitcast(I32))
         nc.sync.dma_start(ww[:], w1_words[0].rearrange("p n t -> p (n t)").bitcast(I32))
         for q in range(QUADS):
-            nc.sync.dma_start(ws[32 * q : 32 * q + 4, :].bitcast(I32), w1_scales[0, 4 * q : 4 * q + 4, :].bitcast(I32))
-        nc.sync.dma_start(l2_sb[:], l2)
-        nc.sync.dma_start(l1_sb[:], l1)
+            load_scales(ws, w1_scales, q)
         nc.sync.dma_start(gs_sb[:], gs.rearrange("(p t) o -> p (t o)", t=PACK))
 
         def dealt(ap):
@@ -65,36 +68,38 @@ def tile_picked_candpair8_none_po_kernel(
         def plain(ap):
             return ap.rearrange("p (m t) -> p m t", t=PACK)
 
-        qs = tile("qs", [P, S], U8)
-        nc.vector.tensor_copy(qs[:], xs[:].indirect(offs_sb[:]))
         cs = tile("cs", [P, S], U8)
         nc.vector.tensor_copy(cs[:], xs[:].indirect(cand_sb[:]))
+        qs = tile("qs", [P, S], U8)
+        nc.vector.tensor_copy(qs[:], xs[:].indirect(offs_sb[:]))
+        csd = tile("csd", [P, S], U8)
+        nc.vector.tensor_copy(dealt(csd[:]), plain(cs[:]))
         qw = tile("qw", [P, S], U32)
         nc.vector.tensor_copy(qw[:], xw[:].bitcast(U32).indirect(offs_sb[:]))
         wwd = tile("wwd", [P, H], I32)
         nc.vector.tensor_copy(dealt(wwd[:]), plain(ww[:]))
         wsd = tile("wsd", [P, H], U8)
         nc.vector.tensor_copy(dealt(wsd[:]), plain(ws[:]))
-        csd = tile("csd", [P, S], U8, tag="ws")
-        nc.vector.tensor_copy(dealt(csd[:]), plain(cs[:]))
-        cw = tile("cw", [P, S], U32, tag="cs")
+        cw = tile("cw", [P, S], U32, tag="ws")
         nc.vector.tensor_copy(dealt(cw[:]), xw[:].bitcast(U32).indirect(cand_sb[:]))
 
         h = []
         for t in range(PACK):
             cols = slice(t * P, (t + 1) * P)
-            acc = psum.tile([P, S], F32, name=f"acc{t}")
-            nc.tensor.matmul_mx(
-                out=acc[:],
-                lhsT=wwd[:, cols].bitcast(FP8X4),
-                lhsT_scale=wsd[:, cols],
-                rhs=qw[:].bitcast(FP8X4),
-                rhs_scale=qs[:],
-                start=True,
-                stop=True,
-            )
             h_t = tile(f"h{t}", [P, S], F32)
-            nc.scalar.activation(h_t[:], acc[:], ACT.Relu)
+            width = S // 2 if t == 0 else S
+            for j in range(0, S, width):
+                acc = psum.tile([P, S], F32, name=f"acc{t}{j}", tag=f"bank{t}" if j == 0 else "bank4")
+                nc.tensor.matmul_mx(
+                    out=acc[:, :width],
+                    lhsT=wwd[:, cols].bitcast(FP8X4),
+                    lhsT_scale=wsd[:, cols],
+                    rhs=qw[:, j : j + width].bitcast(FP8X4),
+                    rhs_scale=qs[:, j : j + width],
+                    start=True,
+                    stop=True,
+                )
+                nc.scalar.activation(h_t[:, j : j + width], acc[:, :width], ACT.Relu)
             h.append(h_t)
 
         out_rows = out_0.rearrange("(p t) v -> p t v", t=PACK)
@@ -112,42 +117,54 @@ def tile_picked_candpair8_none_po_kernel(
                 nc.vector.tensor_tensor(diff[:], h[t][:].indirect(l1_sb[:, entries]), seconds[u][:], ALU.subtract)
                 nc.scalar.activation(zb[u][:, :, t], diff[:], ACT.Copy, scale=gs_sb[:, t : t + 1])
 
-        banks = []
+        def score(acc, t, zw, zs):
+            cols = slice(t * P, (t + 1) * P)
+            nc.tensor.matmul_mx(
+                out=acc,
+                lhsT=cw[:, cols].bitcast(FP8X4),
+                lhsT_scale=csd[:, cols],
+                rhs=zw[:].bitcast(FP8X4),
+                rhs_scale=zs[:],
+                start=True,
+                stop=True,
+            )
+
+        def store_pair(u, pair, zw, zs, dst):
+            acc = psum.tile([P, S], F32, name=f"score{u}{pair}", tag=f"bank{2 * u + pair}")
+            for e in range(2):
+                score(acc[:, e * HALF : (e + 1) * HALF], 2 * pair + e, zw, zs)
+            nc.scalar.activation(dst.rearrange("p e v -> p (e v)"), acc[:, : 2 * HALF], ACT.Copy, scale=OUT_SCALE)
+
+        z = []
         for u in range(2):
             zw = tile(f"zw{u}", [P, HALF], U32)
             zs = tile(f"zs{u}", [P, HALF], U8)
             nc.vector.quantize_mx(out=zw[:].bitcast(FP8X4), scales=zs[:], in_=zb[u][:].rearrange("p v t -> p (v t)"))
-            bank = psum.tile([P, PACK * HALF], F32, name=f"bank{u}")
-            for t in range(PACK):
-                cols = slice(t * P, (t + 1) * P)
-                nc.tensor.matmul_mx(
-                    out=bank[:, t * HALF : (t + 1) * HALF],
-                    lhsT=cw[:, cols].bitcast(FP8X4),
-                    lhsT_scale=csd[:, cols],
-                    rhs=zw[:].bitcast(FP8X4),
-                    rhs_scale=zs[:],
-                    start=True,
-                    stop=True,
-                )
-            banks.append(bank)
+            z.append((zw, zs))
 
-        ow = tile("ow", [P, V], I32)
-        osc = tile("osc", [P, V], U8)
         y0 = tile("y0", [P, PACK, HALF], F32)
-        nc.scalar.activation(y0[:].rearrange("p t v -> p (t v)"), banks[0][:], ACT.Copy, scale=OUT_SCALE)
-        nc.sync.dma_start(out_rows[:, :, :HALF], y0[:])
-        yb1 = tile("yb1", [P, HALF, PACK], BF16)
-        nc.vector.tensor_scalar_mul(yb1[:], banks[1][:].rearrange("p (t v) -> p v t", t=PACK), OUT_SCALE)
         for pair in range(2):
-            y1 = tile(f"y1{pair}", [P, 2, HALF], F32)
-            nc.scalar.activation(y1[:].rearrange("p e v -> p (e v)"), banks[1][:, pair * V : (pair + 1) * V], ACT.Copy, scale=OUT_SCALE)
-            nc.sync.dma_start(out_rows[:, 2 * pair : 2 * pair + 2, HALF:], y1[:])
+            store_pair(0, pair, *z[0], y0[:, 2 * pair : 2 * pair + 2, :])
+        nc.sync.dma_start(out_rows[:, :, :HALF], y0[:])
         yb0 = tile("yb0", [P, HALF, PACK], BF16)
         nc.vector.tensor_copy(yb0[:], y0[:].rearrange("p t v -> p v t"))
-        for u, yb in ((1, yb1), (0, yb0)):
+
+        whole = psum.tile([P, S], F32, name="whole", tag="bank4")
+        for t in range(PACK):
+            score(whole[:, t * HALF : (t + 1) * HALF], t, *z[1])
+        yb1 = tile("yb1", [P, HALF, PACK], BF16)
+        nc.vector.tensor_scalar_mul(yb1[:], whole[:].rearrange("p (t v) -> p v t", t=PACK), OUT_SCALE)
+        for pair in range(2):
+            y1 = tile(f"y1{pair}", [P, 2, HALF], F32)
+            store_pair(1, pair, *z[1], y1[:])
+            nc.sync.dma_start(out_rows[:, 2 * pair : 2 * pair + 2, HALF:], y1[:])
+
+        ow = tile("ow", [P, V], I32, tag="zw1")
+        osc = tile("osc", [P, V], U8)
+        for u, yb in enumerate((yb0, yb1)):
             vcols = slice(u * HALF, (u + 1) * HALF)
             nc.vector.quantize_mx(out=ow[:, vcols].bitcast(FP8X4), scales=osc[:, vcols], in_=yb[:].rearrange("p v t -> p (v t)"))
-        nc.scalar.dma_start(out_1[0].rearrange("p v r -> p (v r)").bitcast(I32), ow[:])
+        nc.sync.dma_start(out_1[0].rearrange("p v r -> p (v r)").bitcast(I32), ow[:])
         for q in range(QUADS):
-            queue = nc.sync if q % 2 == 0 else nc.scalar
+            queue = nc.scalar if q % 2 == 0 else nc.sync
             queue.dma_start(out_2[0, 4 * q : 4 * q + 4, :].bitcast(I32), osc[32 * q : 32 * q + 4, :].bitcast(I32))

from contextlib import ExitStack

import concourse.mybir as mybir

K, T, S, V, H = 512, 2048, 512, 256, 512
FLOPS = 2 * K * H * S + 2 * K * S * V

F32 = mybir.dt.float32
BF16 = mybir.dt.bfloat16
I32 = mybir.dt.int32
U32 = mybir.dt.uint32
U16 = mybir.dt.uint16
U8 = mybir.dt.uint8
FP8X4 = mybir.dt.float8_e4m3fn_x4
ACT = mybir.ActivationFunctionType
ALU = mybir.AluOpType

P = 128
PACK = 4
QUADS = 4
HALF = V // 2
LIST = 16
OUT_SCALE = 0.0625


def tile_picked_candpair8_none_po_kernel(
    tc, x_words, x_scales, w1_words, w1_scales, gs, offs, l1, l2, cand, out_0, out_1, out_2
):
    nc = tc.nc
    with ExitStack() as ctx:
        keep = ctx.enter_context(tc.tile_pool(name="keep", bufs=1))
        psum = ctx.enter_context(tc.psum_pool(name="psum", bufs=1))

        def tile(name, shape, dtype, tag=""):
            return keep.tile(shape, dtype, name=name, tag=tag or name, align_bytes=64)

        offs_sb = tile("offs_sb", [P, S // LIST], U16)
        cand_sb = tile("cand_sb", [P, S // LIST], U16)
        l1_sb = tile("l1_sb", [P, V // LIST], U16)
        l2_sb = tile("l2_sb", [P, V // LIST], U16)
        xw = tile("xw", [P, T], I32)
        xs = tile("xs", [P, T], U8)
        ww = tile("ww", [P, H], I32)
        ws = tile("ws", [P, H], U8)
        gs_sb = tile("gs_sb", [P, PACK], F32)

        nc.vector.memset(xs[:].bitcast(I32), 0)
        nc.vector.memset(ws[:].bitcast(I32), 0)

        def load_scales(plane, rows, q):
            nc.sync.dma_start(plane[32 * q : 32 * q + 4, :].bitcast(I32), rows[0, 4 * q : 4 * q + 4, :].bitcast(I32))

        nc.sync.dma_start(cand_sb[:], cand)
        nc.sync.dma_start(offs_sb[:], offs)
        for q in range(QUADS):
            load_scales(xs, x_scales, q)
        nc.sync.dma_start(l2_sb[:], l2)
        nc.sync.dma_start(l1_sb[:], l1)
        nc.sync.dma_start(xw[:], x_words[0].rearrange("p n t -> p (n t)").bitcast(I32))
        nc.sync.dma_start(ww[:], w1_words[0].rearrange("p n t -> p (n t)").bitcast(I32))
        for q in range(QUADS):
            load_scales(ws, w1_scales, q)
        nc.sync.dma_start(gs_sb[:], gs.rearrange("(p t) o -> p (t o)", t=PACK))

        def dealt(ap):
            return ap.rearrange("p (t m) -> p m t", t=PACK)

        def plain(ap):
            return ap.rearrange("p (m t) -> p m t", t=PACK)

        cs = tile("cs", [P, S], U8)
        nc.vector.tensor_copy(cs[:], xs[:].indirect(cand_sb[:]))
        qs = tile("qs", [P, S], U8)
        nc.vector.tensor_copy(qs[:], xs[:].indirect(offs_sb[:]))
        csd = tile("csd", [P, S], U8)
        nc.vector.tensor_copy(dealt(csd[:]), plain(cs[:]))
        qw = tile("qw", [P, S], U32)
        nc.vector.tensor_copy(qw[:], xw[:].bitcast(U32).indirect(offs_sb[:]))
        wwd = tile("wwd", [P, H], I32)
        nc.vector.tensor_copy(dealt(wwd[:]), plain(ww[:]))
        wsd = tile("wsd", [P, H], U8)
        nc.vector.tensor_copy(dealt(wsd[:]), plain(ws[:]))
        cw = tile("cw", [P, S], U32, tag="ws")
        nc.vector.tensor_copy(dealt(cw[:]), xw[:].bitcast(U32).indirect(cand_sb[:]))

        h = []
        for t in range(PACK):
            cols = slice(t * P, (t + 1) * P)
            h_t = tile(f"h{t}", [P, S], F32)
            width = S // 2 if t == 0 else S
            for j in range(0, S, width):
                acc = psum.tile([P, S], F32, name=f"acc{t}{j}", tag=f"bank{t}" if j == 0 else "bank4")
                nc.tensor.matmul_mx(
                    out=acc[:, :width],
                    lhsT=wwd[:, cols].bitcast(FP8X4),
                    lhsT_scale=wsd[:, cols],
                    rhs=qw[:, j : j + width].bitcast(FP8X4),
                    rhs_scale=qs[:, j : j + width],
                    start=True,
                    stop=True,
                )
                nc.scalar.activation(h_t[:, j : j + width], acc[:, :width], ACT.Relu)
            h.append(h_t)

        out_rows = out_0.rearrange("(p t) v -> p t v", t=PACK)
        zb = [tile(f"zb{u}", [P, HALF, PACK], BF16) for u in range(2)]
        for t in range(PACK):
            seconds = []
            for u in range(2):
                entries = slice(u * HALF // LIST, (u + 1) * HALF // LIST)
                second = tile(f"second{u}{t}", [P, HALF], F32)
                nc.vector.tensor_copy(second[:], h[t][:].indirect(l2_sb[:, entries]))
                seconds.append(second)
            for u in range(2):
                entries = slice(u * HALF // LIST, (u + 1) * HALF // LIST)
                diff = tile(f"diff{u}{t}", [P, HALF], F32)
                nc.vector.tensor_tensor(diff[:], h[t][:].indirect(l1_sb[:, entries]), seconds[u][:], ALU.subtract)
                nc.scalar.activation(zb[u][:, :, t], diff[:], ACT.Copy, scale=gs_sb[:, t : t + 1])

        def score(acc, t, zw, zs):
            cols = slice(t * P, (t + 1) * P)
            nc.tensor.matmul_mx(
                out=acc,
                lhsT=cw[:, cols].bitcast(FP8X4),
                lhsT_scale=csd[:, cols],
                rhs=zw[:].bitcast(FP8X4),
                rhs_scale=zs[:],
                start=True,
                stop=True,
            )

        def store_pair(u, pair, zw, zs, dst):
            acc = psum.tile([P, S], F32, name=f"score{u}{pair}", tag=f"bank{2 * u + pair}")
            for e in range(2):
                score(acc[:, e * HALF : (e + 1) * HALF], 2 * pair + e, zw, zs)
            nc.scalar.activation(dst.rearrange("p e v -> p (e v)"), acc[:, : 2 * HALF], ACT.Copy, scale=OUT_SCALE)

        z = []
        for u in range(2):
            zw = tile(f"zw{u}", [P, HALF], U32)
            zs = tile(f"zs{u}", [P, HALF], U8)
            nc.vector.quantize_mx(out=zw[:].bitcast(FP8X4), scales=zs[:], in_=zb[u][:].rearrange("p v t -> p (v t)"))
            z.append((zw, zs))

        y0 = tile("y0", [P, PACK, HALF], F32)
        for pair in range(2):
            store_pair(0, pair, *z[0], y0[:, 2 * pair : 2 * pair + 2, :])
        nc.sync.dma_start(out_rows[:, :, :HALF], y0[:])
        yb0 = tile("yb0", [P, HALF, PACK], BF16)
        nc.vector.tensor_copy(yb0[:], y0[:].rearrange("p t v -> p v t"))

        whole = psum.tile([P, S], F32, name="whole", tag="bank4")
        for t in range(PACK):
            score(whole[:, t * HALF : (t + 1) * HALF], t, *z[1])
        yb1 = tile("yb1", [P, HALF, PACK], BF16)
        nc.vector.tensor_scalar_mul(yb1[:], whole[:].rearrange("p (t v) -> p v t", t=PACK), OUT_SCALE)
        for pair in range(2):
            y1 = tile(f"y1{pair}", [P, 2, HALF], F32)
            store_pair(1, pair, *z[1], y1[:])
            nc.sync.dma_start(out_rows[:, 2 * pair : 2 * pair + 2, HALF:], y1[:])

        ow = tile("ow", [P, V], I32, tag="zw1")
        osc = tile("osc", [P, V], U8)
        for u, yb in enumerate((yb0, yb1)):
            vcols = slice(u * HALF, (u + 1) * HALF)
            nc.vector.quantize_mx(out=ow[:, vcols].bitcast(FP8X4), scales=osc[:, vcols], in_=yb[:].rearrange("p v t -> p (v t)"))
        nc.sync.dma_start(out_1[0].rearrange("p v r -> p (v r)").bitcast(I32), ow[:])
        for q in range(QUADS):
            queue = nc.scalar if q % 2 == 0 else nc.sync
            queue.dma_start(out_2[0, 4 * q : 4 * q + 4, :].bitcast(I32), osc[32 * q : 32 * q + 4, :].bitcast(I32))
